import numpy as np
import ml_dtypes


def mxq(x, axis, fmt="e4m3"):
    dtype, down = {"e4m3": (ml_dtypes.float8_e4m3fn, 7), "e5m2": (ml_dtypes.float8_e5m2, 14)}[fmt]
    v = np.moveaxis(np.asarray(x, np.float32).astype(ml_dtypes.bfloat16).astype(np.float64), axis, -1)
    blocks = v.reshape(v.shape[:-1] + (-1, 32))
    amax = np.abs(blocks).max(-1, keepdims=True)
    byte = np.maximum(np.where(amax > 0, np.frexp(amax)[1] - 1 + 127, 0) - down, 1)
    scale = np.exp2(byte - 127.0)
    codes = (blocks / scale).astype(np.float32).astype(dtype).astype(np.float64)
    return np.moveaxis((codes * scale).reshape(v.shape), -1, axis)


WIDE = False


def mx_kscale(k):
    if not WIDE:
        return np.ones(k)
    levels = np.array([10, -10, 5, -5, 0])
    if k % 512:
        return np.exp2(np.random.permutation(np.resize(levels, k // 32))).repeat(32)
    a = np.empty((k // 512, 16))
    for p in range(k // 512):
        a[p, :8] = np.random.permutation(np.resize(levels, 8))
        for g in range(8):
            far = levels[np.abs(levels - a[p, g]) >= 10]
            a[p, g + 8] = far[np.random.randint(len(far))]
    return np.exp2(a.ravel()).repeat(32)


def f64(x):
    return np.asarray(x).astype(np.float64)


def striped(idx):
    return np.tile(idx.reshape(-1, 16).T, (8, 1)).astype(np.uint16)


def unstriped(offs):
    return offs[:16].T.reshape(-1).astype(np.int64)


def striped8(idx):
    return np.concatenate([x.reshape(-1, 16).T for x in idx]).astype(np.uint16)


def runs(offs, k):
    lists = np.stack([offs[16 * r : 16 * r + 16].T.reshape(-1) for r in range(8)]).astype(np.int64)
    return lists[np.arange(k) % 512 // 64]


def pack_weight(w):
    k, n = w.shape
    w = f64(np.asarray(w, np.float32).astype(ml_dtypes.bfloat16)).reshape(k // 32, 32, n)
    amax = np.abs(w).max(1)
    byte = np.clip(np.where(amax > 0, np.frexp(amax)[1] - 1 + 127 - 7, 1), 1, 254)
    scaled = (w * np.exp2(127.0 - byte)[:, None, :]).reshape(k, n).astype(np.float32)
    words = np.ascontiguousarray(scaled.reshape(k // 512, 128, 4, n).transpose(0, 1, 3, 2)).astype(ml_dtypes.float8_e4m3fn).view(np.uint8)
    return words, np.ascontiguousarray(byte.astype(np.uint8).reshape(k // 512, 16, n))


def unpack_weight(words, scales):
    g, p, n, _ = words.shape
    vals = np.ascontiguousarray(words).view(ml_dtypes.float8_e4m3fn).astype(np.float64) * np.repeat(np.exp2(scales.astype(np.float64) - 127.0), 8, axis=1)[..., None]
    return vals.transpose(0, 1, 3, 2).reshape(g * 512, n)

def planes(y):
    n, m = y.shape
    v = y.astype(np.float32).astype(ml_dtypes.bfloat16).astype(np.float64).reshape(n // 32, 32, m)
    top = np.abs(v).max(1)
    byte = np.clip(np.where(top > 0, np.frexp(top)[1] - 1 + 127 - 7, 1), 1, 254)
    codes = (v * np.exp2(127.0 - byte)[:, None, :]).reshape(n, m).astype(np.float32).astype(ml_dtypes.float8_e4m3fn).view(np.uint8)
    words = codes.reshape(n // 512, 128, 4, m).transpose(0, 1, 3, 2)
    return np.ascontiguousarray(words), np.ascontiguousarray(byte.astype(np.uint8).reshape(n // 512, 16, m))


K, T, S, G, H, W, U = 512, 1024, 256, 2048, 512, 128, 512


def setup_inputs():
    n = np.random.standard_normal
    s = mx_kscale(K)[:, None]
    packed_xT = pack_weight(n((K, T)) * s)
    packed_dT = pack_weight(n((K, G)) / s)
    perm = np.random.permutation(S)
    perm2 = np.random.permutation(U)
    return {
        "x_words": packed_xT[0],
        "x_scales": packed_xT[1],
        "d_words": packed_dT[0],
        "d_scales": packed_dT[1],
        "gs": (np.random.uniform(0.5, 1.5, (K, 1)) * s).astype(np.float32),
        "offs": striped(np.random.permutation(T)[:S]),
        "ka": striped8(np.random.randint(0, G, (8, H))),
        "kb": striped8(np.random.randint(0, G, (8, H))),
        "n1": striped(perm[:W]),
        "n2": striped(perm[W:]),
        "kc": striped8(np.random.randint(0, G, (8, H))),
        "kd": striped8(np.random.randint(0, G, (8, H))),
        "n3": striped(perm2[:S]),
        "n4": striped(perm2[S:]),
        "n5": striped(np.random.permutation(S)),
        "n6": striped(np.random.permutation(S)),
    }


def reference(x_words, x_scales, d_words, d_scales, gs, offs, ka, kb, n1, n2, kc, kd, n3, n4, n5, n6):
    d_kc = unpack_weight(d_words, d_scales)[np.arange(K)[:, None], runs(kc, K)]
    d_ka = unpack_weight(d_words, d_scales)[np.arange(K)[:, None], runs(ka, K)]
    xq = unpack_weight(x_words, x_scales)[:, unstriped(offs)]
    d_kb = unpack_weight(d_words, d_scales)[np.arange(K)[:, None], runs(kb, K)]
    h = 0.0625 * (d_ka.T @ xq + d_kb.T @ xq)
    pb = h[:, unstriped(n2)]
    pa = h[:, unstriped(n1)]
    rb = pb - (0.5 * pa)
    ra = np.sqrt((pa) ** 2 + (pb) ** 2 + 0.25)
    ua = np.zeros((H, S))
    ua[:, unstriped(n1)] = ra
    ub = ua.copy()
    ub[:, unstriped(n2)] = rb
    z = f64(gs) * ub
    zq = mxq(z, 0, "e4m3")
    d_kd = unpack_weight(d_words, d_scales)[np.arange(K)[:, None], runs(kd, K)]
    h2 = 0.0625 * (d_kc.T @ zq + d_kd.T @ zq)
    st = h2 - h2[:, unstriped(n5)]
    up = np.maximum(st, st[:, unstriped(n6)])
    ph = np.zeros((H, U))
    ph[:, unstriped(n3)] = st
    out = ph.copy()
    out[:, unstriped(n4)] = up
    return (out,) + planes(out)

@@ -1,0 +1,218 @@
+from contextlib import ExitStack
+
+import concourse.mybir as mybir
+
+F32 = mybir.dt.float32
+BF16 = mybir.dt.bfloat16
+I32 = mybir.dt.int32
+U32 = mybir.dt.uint32
+U16 = mybir.dt.uint16
+U8 = mybir.dt.uint8
+FP8X4 = mybir.dt.float8_e4m3fn_x4
+ALU = mybir.AluOpType
+ACT = mybir.ActivationFunctionType
+
+P = 128
+PACK = 4
+K, T, S, G, H, W, U = 512, 1024, 256, 2048, 512, 128, 512
+SPARE = 16
+
+FLOPS = 4 * 2 * K * H * S
+
+
+def tile_picked_atzapolarpagew_none_po_kernel(
+    tc, x_words, x_scales, d_words, d_scales, gs, offs, ka, kb, n1, n2, kc, kd, n3, n4, n5, n6, out_0, out_1, out_2
+):
+    nc = tc.nc
+    with ExitStack() as ctx:
+        keep = ctx.enter_context(tc.tile_pool(name="keep", bufs=1))
+        shared = ctx.enter_context(tc.tile_pool(name="shared", bufs=1))
+        psum = ctx.enter_context(tc.psum_pool(name="psum", bufs=1))
+
+        def tile(name, shape, dtype, tag=None):
+            return keep.tile(shape, dtype, name=name, tag=tag or name, align_bytes=64)
+
+        def load_list(name, src):
+            lst = tile(name, list(src.shape), U16)
+            nc.sync.dma_start(lst[:], src)
+            return lst
+
+        d_bytes = tile("d_bytes", [P, G], U8)
+        x_bytes = tile("x_bytes", [P, T], U8)
+        def load_rows(dst, rows):
+            words = rows.bitcast(I32)
+            nc.scalar.dma_start(dst[:].bitcast(I32), words.unsqueeze(1).broadcast_to([16, 8, words.shape[1]]))
+
+        load_rows(d_bytes, d_scales[0])
+        l_ka = load_list("l_ka", ka)
+        l_kb = load_list("l_kb", kb)
+        l_offs = load_list("l_offs", offs)
+        load_rows(x_bytes, x_scales[0])
+        d_tab = tile("d_tab", [P, G], I32)
+        x_tab = tile("x_tab", [P, T], I32)
+        nc.scalar.dma_start(d_tab[:], d_words[0].rearrange("p n t -> p (n t)").bitcast(I32))
+        nc.scalar.dma_start(x_tab[:], x_words[0].rearrange("p n t -> p (n t)").bitcast(I32))
+        l_n1 = load_list("l_n1", n1)
+        l_n2 = load_list("l_n2", n2)
+        l_kc = load_list("l_kc", kc)
+        l_kd = load_list("l_kd", kd)
+        l_n5 = load_list("l_n5", n5)
+        l_n6 = load_list("l_n6", n6)
+        l_n3 = load_list("l_n3", n3)
+        l_n4 = load_list("l_n4", n4)
+        gain = tile("gain", [P, PACK], F32)
+        nc.gpsimd.dma_start(gain[:], gs.rearrange("(p t) o -> p (t o)", t=PACK))
+
+        placed1 = tile("placed1", [P, 2 * H + S], U8)
+        placed2 = tile("placed2", [P, 2 * H], U8)
+        nc.vector.memset(placed1[:].bitcast(I32), 0)
+        nc.vector.memset(placed2[:].bitcast(I32), 0)
+        h2 = [tile(f"h2_{t}", [P, S + SPARE], F32) for t in range(PACK)]
+        st = [tile(f"st_{t}", [P, S + SPARE], F32) for t in range(PACK)]
+        for t in range(PACK):
+            nc.vector.memset(h2[t][:, S:], 0.0)
+            nc.vector.memset(st[t][:, S:], 0.0)
+
+        def gather(out, window, lst):
+            nc.vector.tensor_copy(out, window.indirect(lst[:]))
+
+        def place(picked, placed, queues):
+            for q in range(4):
+                queues[q % len(queues)].dma_start(
+                    placed[32 * q : 32 * q + 4, :].bitcast(I32), picked[32 * q : 32 * q + 32 : 8, :].bitcast(I32)
+                )
+
+        def deal(t0, t1, words, placed, name):
+            w = tile(f"{name}_w{t0}", [P, t1 - t0, 2 * P], U32)
+            b = tile(f"{name}_b{t0}", [P, t1 - t0, 2 * P], U8)
+            for dst, src in ((w, words[:]), (b, placed[:, : 2 * H])):
+                nc.vector.tensor_copy(dst[:].rearrange("p t m -> p m t"), src.rearrange("p (m t) -> p m t", t=PACK)[:, :, t0:t1])
+            return [(w[:, t, :], b[:, t, :]) for t in range(t1 - t0)]
+
+        def product(name, w, b, rhs_w, rhs_b):
+            acc = psum.tile([P, S], F32, name=name, tag=name)
+            for l in range(2):
+                nc.tensor.matmul_mx(
+                    out=acc[:], lhsT=w[:, l * P : (l + 1) * P].bitcast(FP8X4), lhsT_scale=b[:, l * P : (l + 1) * P],
+                    rhs=rhs_w.bitcast(FP8X4), rhs_scale=rhs_b, start=(l == 0), stop=(l == 1),
+                )
+            return acc
+
+        picked_b1 = tile("picked_b1", [P, 2 * H + S], U8)
+        gather(picked_b1[:, 0:H], d_bytes[:], l_ka)
+        gather(picked_b1[:, H : 2 * H], d_bytes[:], l_kb)
+        gather(picked_b1[:, 2 * H :], x_bytes[:], l_offs)
+        place(picked_b1, placed1, [nc.sync])
+        picked_w1 = tile("picked_w1", [P, 2 * H], U32)
+        x_picked = tile("x_picked", [P, S], U32)
+        gather(picked_w1[:, 0:H], d_tab[:].bitcast(U32), l_ka)
+        gather(picked_w1[:, H:], d_tab[:].bitcast(U32), l_kb)
+        gather(x_picked[:], x_tab[:].bitcast(U32), l_offs)
+
+        accs = []
+        for t0, t1 in ((0, 1), (1, 2), (2, 4)):
+            for t, (w, b) in enumerate(deal(t0, t1, picked_w1, placed1, "first"), t0):
+                accs.append(product(f"acc1_{t}", w, b, x_picked[:], placed1[:, 2 * H :]))
+        h = [tile(f"h_{t}", [P, S], F32) for t in range(PACK)]
+        pab = [tile(f"pab_{t}", [P, 2 * W], F32) for t in range(PACK)]
+        rb = [tile(f"rb_{t}", [P, W], F32) for t in range(PACK)]
+        ra = [tile(f"ra_{t}", [P, W], F32) for t in range(PACK)]
+        ssum = [tile(f"ssum_{t}", [P, W], F32) for t in range(PACK)]
+        ub = [tile(f"ub_{t}", [P, S], F32) for t in range(PACK)]
+        sq = [shared.tile([P, 2 * W], F32, name=f"sq_{t}", offset=1024 * t, align_bytes=64) for t in range(PACK)]
+        for t in range(PACK):
+            if t < 2:
+                nc.scalar.activation(h[t][:], accs[t][:], ACT.Copy, scale=0.0625)
+            else:
+                nc.vector.tensor_scalar(h[t][:], accs[t][:], 0.0625, None, ALU.mult)
+            nc.scalar.activation(pab[t][:, :W], h[t][:].indirect(l_n1[:]), ACT.Copy)
+            nc.scalar.activation(pab[t][:, W:], h[t][:].indirect(l_n2[:]), ACT.Copy)
+        for t in range(PACK):
+            nc.vector.tensor_tensor(sq[t][:], pab[t][:], pab[t][:], ALU.mult)
+            nc.vector.scalar_tensor_tensor(rb[t][:], pab[t][:, :W], -0.5, pab[t][:, W:], ALU.mult, ALU.add)
+            nc.vector.scalar_tensor_tensor(ssum[t][:], sq[t][:, :W], 0.25, sq[t][:, W:], ALU.add, ALU.add)
+
+        picked_b2 = shared.tile([P, 2 * H], U8, name="picked_b2", offset=2048, align_bytes=64)
+        gather(picked_b2[:, 0:H], d_bytes[:], l_kc)
+        gather(picked_b2[:, H:], d_bytes[:], l_kd)
+        place(picked_b2, placed2, [nc.sync])
+
+        z_bf = tile("z_bf", [P, S, PACK], BF16)
+
+        def scatter(window, lst, values):
+            nc.scalar.activation(window[:].indirect(lst[:]), values, ACT.Copy)
+
+        def finish_z(t):
+            scatter(ub[t], l_n1, ra[t][:])
+            nc.vector.tensor_scalar(z_bf[:, :, t], ub[t][:], gain[:, t : t + 1], None, ALU.mult)
+
+        picked_w2 = shared.tile([P, 2 * H], U32, name="picked_w2", offset=3072, align_bytes=64)
+        gather(picked_w2[:, 0:H], d_tab[:].bitcast(U32), l_kc)
+        gather(picked_w2[:, H:], d_tab[:].bitcast(U32), l_kd)
+        for t in range(PACK):
+            scatter(ub[t], l_n2, rb[t][:])
+            if t > 0:
+                finish_z(t - 1)
+            nc.scalar.activation(ra[t][:], ssum[t][:], ACT.Sqrt)
+        second = deal(0, 1, picked_w2, placed2, "second")
+        finish_z(PACK - 1)
+
+        z_w = tile("z_w", [P, S], U32)
+        z_b = tile("z_b", [P, S], U8)
+        nc.vector.quantize_mx(out=z_w[:].bitcast(FP8X4), scales=z_b[:], in_=z_bf[:].rearrange("p s t -> p (s t)"))
+
+        second = second + deal(1, 2, picked_w2, placed2, "second") + deal(2, 4, picked_w2, placed2, "second")
+        far = [tile(f"far_{t}", [P, S], F32) for t in range(PACK)]
+        other = [tile(f"other_{t}", [P, S], F32) for t in range(PACK)]
+        up = [tile(f"up_{t}", [P, S], F32) for t in range(PACK)]
+        page = [tile(f"page_{t}", [P, U], F32) for t in range(PACK)]
+        out_bf = tile("out_bf", [P, U, PACK], BF16)
+        out_rows = out_0.rearrange("(p t) c -> p t c", t=PACK)
+        for t in range(PACK):
+            acc = product(f"acc2_{t}", second[t][0], second[t][1], z_w[:], z_b[:])
+            if t == 0:
+                nc.scalar.activation(h2[t][:, :S], acc[:], ACT.Copy, scale=0.0625)
+            else:
+                nc.vector.tensor_scalar(h2[t][:, :S], acc[:], 0.0625, None, ALU.mult)
+
+        def make_st(t):
+            nc.scalar.activation(far[t][:], h2[t][:].indirect(l_n5[:]), ACT.Copy)
+            nc.vector.tensor_tensor(st[t][:, :S], h2[t][:, :S], far[t][:], ALU.subtract)
+
+        def make_up(t):
+            nc.scalar.activation(other[t][:], st[t][:].indirect(l_n6[:]), ACT.Copy)
+            nc.vector.tensor_tensor(up[t][:], st[t][:, :S], other[t][:], ALU.max)
+            scatter(page[t], l_n3, st[t][:, :S])
+
+        def finish_page(t, pieces):
+            scatter(page[t], l_n4, up[t][:])
+            nc.sync.dma_start(out_rows[:, t, :], page[t][:])
+            step = U // pieces
+            for c in range(0, U, step):
+                nc.vector.tensor_copy(out_bf[:, c : c + step, t], page[t][:, c : c + step])
+
+        make_st(0)
+        make_st(1)
+        make_up(0)
+        make_st(2)
+        finish_page(0, 1)
+        make_up(1)
+        make_st(3)
+        finish_page(1, 1)
+        make_up(2)
+        make_up(3)
+        finish_page(2, 1)
+        finish_page(3, 2)
+
+        out_w = tile("out_w", [P, U], U32)
+        out_b = tile("out_b", [P, U], U8)
+        words_dram = out_1[0].rearrange("p n t -> p (n t)").bitcast(I32)
+        half = U // 2
+        for c in range(0, U, half):
+            nc.vector.quantize_mx(
+                out=out_w[:, c : c + half].bitcast(FP8X4), scales=out_b[:, c : c + half],
+                in_=out_bf[:, c : c + half, :].rearrange("p s t -> p (s t)"),
+            )
+            nc.sync.dma_start(words_dram[:, c : c + half], out_w[:, c : c + half].bitcast(I32))
+        for q in range(4):
+            nc.scalar.dma_start(out_2[0, 4 * q : 4 * q + 4, :].bitcast(I32), out_b[32 * q : 32 * q + 4, :].bitcast(I32))

@@ -15,7 +15,9 @@ ACT = mybir.ActivationFunctionType
 P = 128
 PACK = 4
 K, T, S, G, H, W, U = 512, 1024, 256, 2048, 512, 128, 512
+HALF = H // 2
 SPARE = 16
+KIB = 1024
 
 FLOPS = 4 * 2 * K * H * S
 
@@ -29,39 +31,44 @@ def tile_picked_atzapolarpagew_none_po_kernel(
         shared = ctx.enter_context(tc.tile_pool(name="shared", bufs=1))
         psum = ctx.enter_context(tc.psum_pool(name="psum", bufs=1))
 
-        def tile(name, shape, dtype, tag=None):
-            return keep.tile(shape, dtype, name=name, tag=tag or name, align_bytes=64)
+        def tile(name, shape, dtype, kib=None):
+            if kib is None:
+                return keep.tile(shape, dtype, name=name, align_bytes=64)
+            return shared.tile(shape, dtype, name=name, offset=int(kib * KIB), align_bytes=64)
 
         def load_list(name, src):
             lst = tile(name, list(src.shape), U16)
             nc.sync.dma_start(lst[:], src)
             return lst
 
-        d_bytes = tile("d_bytes", [P, G], U8)
-        x_bytes = tile("x_bytes", [P, T], U8)
-        def load_rows(dst, rows):
+        def load_rows(name, rows):
+            dst = tile(name, [P, rows.shape[1]], U8)
             words = rows.bitcast(I32)
-            nc.scalar.dma_start(dst[:].bitcast(I32), words.unsqueeze(1).broadcast_to([16, 8, words.shape[1]]))
+            nc.sync.dma_start(dst[:].bitcast(I32), words.unsqueeze(1).broadcast_to([16, 8, words.shape[1]]))
+            return dst
 
-        load_rows(d_bytes, d_scales[0])
+        def load_words(name, words):
+            dst = tile(name, [P, words.shape[1]], I32)
+            nc.sync.dma_start(dst[:], words.rearrange("p n t -> p (n t)").bitcast(I32))
+            return dst
+
         l_ka = load_list("l_ka", ka)
+        d_bytes = load_rows("d_bytes", d_scales[0])
         l_kb = load_list("l_kb", kb)
+        x_bytes = load_rows("x_bytes", x_scales[0])
         l_offs = load_list("l_offs", offs)
-        load_rows(x_bytes, x_scales[0])
-        d_tab = tile("d_tab", [P, G], I32)
-        x_tab = tile("x_tab", [P, T], I32)
-        nc.scalar.dma_start(d_tab[:], d_words[0].rearrange("p n t -> p (n t)").bitcast(I32))
-        nc.scalar.dma_start(x_tab[:], x_words[0].rearrange("p n t -> p (n t)").bitcast(I32))
+        x_tab = load_words("x_tab", x_words[0])
+        d_tab = load_words("d_tab", d_words[0])
         l_n1 = load_list("l_n1", n1)
         l_n2 = load_list("l_n2", n2)
         l_kc = load_list("l_kc", kc)
         l_kd = load_list("l_kd", kd)
+        gain = tile("gain", [P, PACK], F32)
+        nc.sync.dma_start(gain[:], gs.rearrange("(p t) o -> p (t o)", t=PACK))
         l_n5 = load_list("l_n5", n5)
         l_n6 = load_list("l_n6", n6)
         l_n3 = load_list("l_n3", n3)
         l_n4 = load_list("l_n4", n4)
-        gain = tile("gain", [P, PACK], F32)
-        nc.gpsimd.dma_start(gain[:], gs.rearrange("(p t) o -> p (t o)", t=PACK))
 
         placed1 = tile("placed1", [P, 2 * H + S], U8)
         placed2 = tile("placed2", [P, 2 * H], U8)
@@ -73,135 +80,183 @@ def tile_picked_atzapolarpagew_none_po_kernel(
             nc.vector.memset(h2[t][:, S:], 0.0)
             nc.vector.memset(st[t][:, S:], 0.0)
 
-        def gather(out, window, lst):
-            nc.vector.tensor_copy(out, window.indirect(lst[:]))
+        def pick(out, window, offsets):
+            nc.vector.tensor_copy(out, window.indirect(offsets))
 
-        def place(picked, placed, queues):
+        def pick_words(picked, u, lists):
+            for l, lst in enumerate(lists):
+                pick(picked[:, l * HALF : (l + 1) * HALF], d_tab[:].bitcast(U32), lst[:, 16 * u : 16 * (u + 1)])
+
+        def place(picked, placed, queue):
             for q in range(4):
-                queues[q % len(queues)].dma_start(
+                queue.dma_start(
                     placed[32 * q : 32 * q + 4, :].bitcast(I32), picked[32 * q : 32 * q + 32 : 8, :].bitcast(I32)
                 )
 
-        def deal(t0, t1, words, placed, name):
-            w = tile(f"{name}_w{t0}", [P, t1 - t0, 2 * P], U32)
-            b = tile(f"{name}_b{t0}", [P, t1 - t0, 2 * P], U8)
-            for dst, src in ((w, words[:]), (b, placed[:, : 2 * H])):
-                nc.vector.tensor_copy(dst[:].rearrange("p t m -> p m t"), src.rearrange("p (m t) -> p m t", t=PACK)[:, :, t0:t1])
-            return [(w[:, t, :], b[:, t, :]) for t in range(t1 - t0)]
+        def deal_low(name, u, picked, placed):
+            w = tile(f"{name}_w{u}", [P, 2, P], U32)
+            b = tile(f"{name}_b{u}", [P, 2, P], U8)
+            words = picked[:].rearrange("p (l m t) -> p l m t", l=2, t=PACK)
+            scales = placed[:, : 2 * H].rearrange("p (l u m t) -> p u l m t", l=2, u=2, t=PACK)[:, u]
+            for dst, src in ((w, words), (b, scales)):
+                nc.vector.tensor_copy(dst[:].rearrange("p l (t m) -> p l m t", t=2), src[:, :, :, 0:2])
+            return w[:], b[:]
 
-        def product(name, w, b, rhs_w, rhs_b):
-            acc = psum.tile([P, S], F32, name=name, tag=name)
+        def deal_high(name, picked, placed, kib=None):
+            w = tile(f"{name}_w23", [P, 2, 2, P], U32, kib)
+            b = tile(f"{name}_b23", [P, 2, 2, P], U8, kib and kib - 0.5)
+            for u in range(2):
+                words = picked[u][:].rearrange("p (l m t) -> p l m t", l=2, t=PACK)
+                nc.vector.tensor_copy(w[:, :, :, 64 * u : 64 * (u + 1)].rearrange("p t l m -> p l m t"), words[:, :, :, 2:4])
+            scales = placed[:, : 2 * H].rearrange("p (m t) -> p m t", t=PACK)
+            nc.vector.tensor_copy(b[:].rearrange("p t l m -> p (l m) t"), scales[:, :, 2:4])
+            return [(w[:, t], b[:, t]) for t in range(2)]
+
+        def product(name, stationary, rhs_w, rhs_b):
+            w, b = stationary
+            acc = psum.tile([P, S], F32, name=name)
             for l in range(2):
                 nc.tensor.matmul_mx(
-                    out=acc[:], lhsT=w[:, l * P : (l + 1) * P].bitcast(FP8X4), lhsT_scale=b[:, l * P : (l + 1) * P],
+                    out=acc[:], lhsT=w[:, l, :].bitcast(FP8X4), lhsT_scale=b[:, l, :],
                     rhs=rhs_w.bitcast(FP8X4), rhs_scale=rhs_b, start=(l == 0), stop=(l == 1),
                 )
             return acc
 
-        picked_b1 = tile("picked_b1", [P, 2 * H + S], U8)
-        gather(picked_b1[:, 0:H], d_bytes[:], l_ka)
-        gather(picked_b1[:, H : 2 * H], d_bytes[:], l_kb)
-        gather(picked_b1[:, 2 * H :], x_bytes[:], l_offs)
-        place(picked_b1, placed1, [nc.sync])
-        picked_w1 = tile("picked_w1", [P, 2 * H], U32)
-        x_picked = tile("x_picked", [P, S], U32)
-        gather(picked_w1[:, 0:H], d_tab[:].bitcast(U32), l_ka)
-        gather(picked_w1[:, H:], d_tab[:].bitcast(U32), l_kb)
-        gather(x_picked[:], x_tab[:].bitcast(U32), l_offs)
+        def sixteenth(dst, acc, on_scalar):
+            if on_scalar:
+                nc.scalar.activation(dst, acc[:], ACT.Copy, scale=0.0625)
+            else:
+                nc.vector.tensor_scalar(dst, acc[:], 0.0625, None, ALU.mult)
 
-        accs = []
-        for t0, t1 in ((0, 1), (1, 2), (2, 4)):
-            for t, (w, b) in enumerate(deal(t0, t1, picked_w1, placed1, "first"), t0):
-                accs.append(product(f"acc1_{t}", w, b, x_picked[:], placed1[:, 2 * H :]))
+        def fetch(out, window, offsets):
+            nc.scalar.activation(out, window[:].indirect(offsets), ACT.Copy)
+
+        def scatter(window, lst, values):
+            nc.scalar.activation(window[:].indirect(lst[:]), values, ACT.Copy)
+
+        def swap_halves(u, src, planes):
+            for j in range(2):
+                nc.sync.dma_start(planes[64 * u : 64 * (u + 1), j, :], src[64 * j : 64 * (j + 1), :])
+
+        picked_b1 = tile("picked_b1", [P, 2 * H + S], U8, 0)
+        pick(picked_b1[:, 0:H], d_bytes[:], l_ka[:])
+        pick(picked_b1[:, H : 2 * H], d_bytes[:], l_kb[:])
+        pick(picked_b1[:, 2 * H :], x_bytes[:], l_offs[:])
+        place(picked_b1, placed1, nc.scalar)
+        x_picked = tile("x_picked", [P, S], U32)
+        pick(x_picked[:], x_tab[:].bitcast(U32), l_offs[:])
+        picked_w1 = [tile("picked_w1_0", [P, H], U32), tile("picked_w1_1", [P, H], U32, 0)]
+        acc1 = []
+        for u in range(2):
+            pick_words(picked_w1[u], u, (l_ka, l_kb))
+            acc1.append(product(f"acc1_{u}", deal_low("first", u, picked_w1[u], placed1), x_picked[:], placed1[:, 2 * H :]))
+        for t, stationary in enumerate(deal_high("first", picked_w1, placed1), 2):
+            acc1.append(product(f"acc1_{t}", stationary, x_picked[:], placed1[:, 2 * H :]))
+
         h = [tile(f"h_{t}", [P, S], F32) for t in range(PACK)]
         pab = [tile(f"pab_{t}", [P, 2 * W], F32) for t in range(PACK)]
         rb = [tile(f"rb_{t}", [P, W], F32) for t in range(PACK)]
         ra = [tile(f"ra_{t}", [P, W], F32) for t in range(PACK)]
         ssum = [tile(f"ssum_{t}", [P, W], F32) for t in range(PACK)]
-        ub = [tile(f"ub_{t}", [P, S], F32) for t in range(PACK)]
-        sq = [shared.tile([P, 2 * W], F32, name=f"sq_{t}", offset=1024 * t, align_bytes=64) for t in range(PACK)]
+        sq = [tile(f"sq_{t}", [P, 2 * W], F32, (2, 4, 6, 34)[t]) for t in range(PACK)]
+        ub = [tile(f"ub_{t}", [P, S], F32, (10, 11, 15, 16)[t]) for t in range(PACK)]
         for t in range(PACK):
-            if t < 2:
-                nc.scalar.activation(h[t][:], accs[t][:], ACT.Copy, scale=0.0625)
-            else:
-                nc.vector.tensor_scalar(h[t][:], accs[t][:], 0.0625, None, ALU.mult)
-            nc.scalar.activation(pab[t][:, :W], h[t][:].indirect(l_n1[:]), ACT.Copy)
-            nc.scalar.activation(pab[t][:, W:], h[t][:].indirect(l_n2[:]), ACT.Copy)
-        for t in range(PACK):
+            sixteenth(h[t][:], acc1[t], t < 2)
+            fetch(pab[t][:, :W], h[t], l_n1[:])
+            fetch(pab[t][:, W:], h[t], l_n2[:])
+
+        def polar(t):
             nc.vector.tensor_tensor(sq[t][:], pab[t][:], pab[t][:], ALU.mult)
             nc.vector.scalar_tensor_tensor(rb[t][:], pab[t][:, :W], -0.5, pab[t][:, W:], ALU.mult, ALU.add)
             nc.vector.scalar_tensor_tensor(ssum[t][:], sq[t][:, :W], 0.25, sq[t][:, W:], ALU.add, ALU.add)
 
-        picked_b2 = shared.tile([P, 2 * H], U8, name="picked_b2", offset=2048, align_bytes=64)
-        gather(picked_b2[:, 0:H], d_bytes[:], l_kc)
-        gather(picked_b2[:, H:], d_bytes[:], l_kd)
-        place(picked_b2, placed2, [nc.sync])
+        polar(0)
+        polar(1)
+        picked_b2 = tile("picked_b2", [P, 2 * H], U8, 4)
+        pick(picked_b2[:, 0:H], d_bytes[:], l_kc[:])
+        pick(picked_b2[:, H:], d_bytes[:], l_kd[:])
+        place(picked_b2, placed2, nc.sync)
+        polar(2)
+        polar(3)
+        picked_w2 = tile("picked_w2", [P, 2 * H], U32, 34)
+        pick(picked_w2[:, 0:H], d_tab[:].bitcast(U32), l_kc[:])
+        pick(picked_w2[:, H:], d_tab[:].bitcast(U32), l_kd[:])
 
-        z_bf = tile("z_bf", [P, S, PACK], BF16)
+        def deal(t0, t1, kib=None):
+            w = tile(f"second_w{t0}", [P, t1 - t0, 2, P], U32, kib)
+            b = tile(f"second_b{t0}", [P, t1 - t0, 2, P], U8, kib and kib - 0.5)
+            for dst, src in ((w, picked_w2), (b, placed2)):
+                nc.vector.tensor_copy(
+                    dst[:].rearrange("p t l m -> p (l m) t"), src[:].rearrange("p (m t) -> p m t", t=PACK)[:, :, t0:t1]
+                )
+            return [(w[:, t], b[:, t]) for t in range(t1 - t0)]
 
-        def scatter(window, lst, values):
-            nc.scalar.activation(window[:].indirect(lst[:]), values, ACT.Copy)
+        second = deal(0, 1)
+
+        ub_low = tile("ub_low", [P, 2, S], F32)
+        z_bf = tile("z_bf", [P, S, PACK], BF16, 10)
 
         def finish_z(t):
             scatter(ub[t], l_n1, ra[t][:])
-            nc.vector.tensor_scalar(z_bf[:, :, t], ub[t][:], gain[:, t : t + 1], None, ALU.mult)
+            if t < 2:
+                swap_halves(t, ub[t], ub_low)
+            for j in ((), (0, 1), (2,), (3,))[t]:
+                rows = ub_low[:, j, :] if j < 2 else ub[j][:]
+                nc.vector.tensor_scalar(z_bf[:, :, j], rows, gain[:, j : j + 1], None, ALU.mult)
 
-        picked_w2 = shared.tile([P, 2 * H], U32, name="picked_w2", offset=3072, align_bytes=64)
-        gather(picked_w2[:, 0:H], d_tab[:].bitcast(U32), l_kc)
-        gather(picked_w2[:, H:], d_tab[:].bitcast(U32), l_kd)
         for t in range(PACK):
-            scatter(ub[t], l_n2, rb[t][:])
+            nc.scalar.activation(ra[t][:], ssum[t][:], ACT.Sqrt)
             if t > 0:
                 finish_z(t - 1)
-            nc.scalar.activation(ra[t][:], ssum[t][:], ACT.Sqrt)
-        second = deal(0, 1, picked_w2, placed2, "second")
+            scatter(ub[t], l_n2, rb[t][:])
         finish_z(PACK - 1)
 
         z_w = tile("z_w", [P, S], U32)
         z_b = tile("z_b", [P, S], U8)
         nc.vector.quantize_mx(out=z_w[:].bitcast(FP8X4), scales=z_b[:], in_=z_bf[:].rearrange("p s t -> p (s t)"))
 
-        second = second + deal(1, 2, picked_w2, placed2, "second") + deal(2, 4, picked_w2, placed2, "second")
         far = [tile(f"far_{t}", [P, S], F32) for t in range(PACK)]
         other = [tile(f"other_{t}", [P, S], F32) for t in range(PACK)]
         up = [tile(f"up_{t}", [P, S], F32) for t in range(PACK)]
         page = [tile(f"page_{t}", [P, U], F32) for t in range(PACK)]
         out_bf = tile("out_bf", [P, U, PACK], BF16)
         out_rows = out_0.rearrange("(p t) c -> p t c", t=PACK)
-        for t in range(PACK):
-            acc = product(f"acc2_{t}", second[t][0], second[t][1], z_w[:], z_b[:])
-            if t == 0:
-                nc.scalar.activation(h2[t][:, :S], acc[:], ACT.Copy, scale=0.0625)
-            else:
-                nc.vector.tensor_scalar(h2[t][:, :S], acc[:], 0.0625, None, ALU.mult)
 
-        def make_st(t):
-            nc.scalar.activation(far[t][:], h2[t][:].indirect(l_n5[:]), ACT.Copy)
-            nc.vector.tensor_tensor(st[t][:, :S], h2[t][:, :S], far[t][:], ALU.subtract)
+        def make_h2(t):
+            sixteenth(h2[t][:, :S], product(f"acc2_{t}", second[t], z_w[:], z_b[:]), t == 0)
+
+        def make_st(t, pieces=1):
+            step = S // pieces
+            for c in range(0, S, step):
+                fetch(far[t][:, c : c + step], h2[t], l_n5[:, c // 16 : (c + step) // 16])
+                nc.vector.tensor_tensor(st[t][:, c : c + step], h2[t][:, c : c + step], far[t][:, c : c + step], ALU.subtract)
 
         def make_up(t):
-            nc.scalar.activation(other[t][:], st[t][:].indirect(l_n6[:]), ACT.Copy)
+            fetch(other[t][:], st[t], l_n6[:])
             nc.vector.tensor_tensor(up[t][:], st[t][:, :S], other[t][:], ALU.max)
             scatter(page[t], l_n3, st[t][:, :S])
 
-        def finish_page(t, pieces):
+        def finish_page(t, pieces=1):
             scatter(page[t], l_n4, up[t][:])
             nc.sync.dma_start(out_rows[:, t, :], page[t][:])
             step = U // pieces
             for c in range(0, U, step):
                 nc.vector.tensor_copy(out_bf[:, c : c + step, t], page[t][:, c : c + step])
 
+        second.extend(deal(1, 2, 10.5) + deal(2, 4, 12))
+        for t in range(PACK):
+            make_h2(t)
         make_st(0)
         make_st(1)
         make_up(0)
         make_st(2)
-        finish_page(0, 1)
+        finish_page(0)
         make_up(1)
         make_st(3)
-        finish_page(1, 1)
+        finish_page(1)
         make_up(2)
         make_up(3)
-        finish_page(2, 1)
+        finish_page(2)
         finish_page(3, 2)
 
         out_w = tile("out_w", [P, U], U32)
@@ -215,4 +270,4 @@ def tile_picked_atzapolarpagew_none_po_kernel(
             )
             nc.sync.dma_start(words_dram[:, c : c + half], out_w[:, c : c + half].bitcast(I32))
         for q in range(4):
-            nc.scalar.dma_start(out_2[0, 4 * q : 4 * q + 4, :].bitcast(I32), out_b[32 * q : 32 * q + 4, :].bitcast(I32))
+            (nc.scalar, nc.sync)[q // 3].dma_start(out_2[0, 4 * q : 4 * q + 4, :].bitcast(I32), out_b[32 * q : 32 * q + 4, :].bitcast(I32))

@@ -70,6 +70,11 @@ def tile_picked_atzapolarpagew_none_po_kernel(
         l_n3 = load_list("l_n3", n3)
         l_n4 = load_list("l_n4", n4)
 
+        warm_in = tile("warm_in", [P, 1], F32)
+        warm_out = tile("warm_out", [P, 1], F32)
+        nc.vector.memset(warm_in[:], 1.0)
+        nc.scalar.activation(warm_out[:], warm_in[:], ACT.Sqrt)
+
         placed1 = tile("placed1", [P, 2 * H + S], U8)
         placed2 = tile("placed2", [P, 2 * H], U8)
         nc.vector.memset(placed1[:].bitcast(I32), 0)

@@ -75,6 +75,8 @@ def tile_picked_atzapolarpagew_none_po_kernel(
         nc.vector.memset(warm_in[:], 1.0)
         nc.scalar.activation(warm_out[:], warm_in[:], ACT.Sqrt)
 
+        quarter = tile("quarter", [P, 1], F32)
+        nc.vector.memset(quarter[:], 0.25)
         placed1 = tile("placed1", [P, 2 * H + S], U8)
         placed2 = tile("placed2", [P, 2 * H], U8)
         nc.vector.memset(placed1[:].bitcast(I32), 0)
@@ -117,9 +119,9 @@ def tile_picked_atzapolarpagew_none_po_kernel(
             nc.vector.tensor_copy(b[:].rearrange("p t l m -> p (l m) t"), scales[:, :, 2:4])
             return [(w[:, t], b[:, t]) for t in range(2)]
 
-        def product(name, stationary, rhs_w, rhs_b):
+        def product(name, stationary, rhs_w, rhs_b, bank=None):
             w, b = stationary
-            acc = psum.tile([P, S], F32, name=name)
+            acc = psum.tile([P, rhs_w.shape[1]], F32, name=name, tag=bank or name)
             for l in range(2):
                 nc.tensor.matmul_mx(
                     out=acc[:], lhsT=w[:, l, :].bitcast(FP8X4), lhsT_scale=b[:, l, :],
@@ -159,11 +161,11 @@ def tile_picked_atzapolarpagew_none_po_kernel(
             acc1.append(product(f"acc1_{t}", stationary, x_picked[:], placed1[:, 2 * H :]))
 
         h = [tile(f"h_{t}", [P, S], F32) for t in range(PACK)]
-        pab = [tile(f"pab_{t}", [P, 2 * W], F32) for t in range(PACK)]
+        pab = [tile(f"pab_{t}", [P, 2 * W], F32, (2, 4, 6, 34)[t]) for t in range(PACK)]
         rb = [tile(f"rb_{t}", [P, W], F32) for t in range(PACK)]
         ra = [tile(f"ra_{t}", [P, W], F32) for t in range(PACK)]
         ssum = [tile(f"ssum_{t}", [P, W], F32) for t in range(PACK)]
-        sq = [tile(f"sq_{t}", [P, 2 * W], F32, (2, 4, 6, 34)[t]) for t in range(PACK)]
+        sq = [tile(f"sq_{t}", [P, 2 * W], F32) for t in range(PACK)]
         ub = [tile(f"ub_{t}", [P, S], F32, (10, 11, 15, 16)[t]) for t in range(PACK)]
         for t in range(PACK):
             sixteenth(h[t][:], acc1[t], t < 2)
@@ -171,9 +173,9 @@ def tile_picked_atzapolarpagew_none_po_kernel(
             fetch(pab[t][:, W:], h[t], l_n2[:])
 
         def polar(t):
-            nc.vector.tensor_tensor(sq[t][:], pab[t][:], pab[t][:], ALU.mult)
             nc.vector.scalar_tensor_tensor(rb[t][:], pab[t][:, :W], -0.5, pab[t][:, W:], ALU.mult, ALU.add)
-            nc.vector.scalar_tensor_tensor(ssum[t][:], sq[t][:, :W], 0.25, sq[t][:, W:], ALU.add, ALU.add)
+            nc.gpsimd.tensor_tensor(sq[t][:], pab[t][:], pab[t][:], ALU.mult)
+            nc.gpsimd.tensor_tensor(ssum[t][:], sq[t][:, :W], sq[t][:, W:], ALU.add)
 
         polar(0)
         polar(1)
@@ -187,9 +189,9 @@ def tile_picked_atzapolarpagew_none_po_kernel(
         pick(picked_w2[:, 0:H], d_tab[:].bitcast(U32), l_kc[:])
         pick(picked_w2[:, H:], d_tab[:].bitcast(U32), l_kd[:])
 
-        def deal(t0, t1, kib=None):
-            w = tile(f"second_w{t0}", [P, t1 - t0, 2, P], U32, kib)
-            b = tile(f"second_b{t0}", [P, t1 - t0, 2, P], U8, kib and kib - 0.5)
+        def deal(t0, t1, kib=None, kib_b=None):
+            w = tile(f"second_w{t0}", [P, t1 - t0, 2, P], U32, kib and kib + 0.25)
+            b = tile(f"second_b{t0}", [P, t1 - t0, 2, P], U8, kib_b)
             for dst, src in ((w, picked_w2), (b, placed2)):
                 nc.vector.tensor_copy(
                     dst[:].rearrange("p t l m -> p (l m) t"), src[:].rearrange("p (m t) -> p m t", t=PACK)[:, :, t0:t1]
@@ -198,6 +200,7 @@ def tile_picked_atzapolarpagew_none_po_kernel(
 
         second = deal(0, 1)
 
+        halves = [slice(0, S // 2), slice(S // 2, S)]
         ub_low = tile("ub_low", [P, 2, S], F32)
         z_bf = tile("z_bf", [P, S, PACK], BF16, 10)
 
@@ -207,18 +210,22 @@ def tile_picked_atzapolarpagew_none_po_kernel(
                 swap_halves(t, ub[t], ub_low)
             for j in ((), (0, 1), (2,), (3,))[t]:
                 rows = ub_low[:, j, :] if j < 2 else ub[j][:]
-                nc.vector.tensor_scalar(z_bf[:, :, j], rows, gain[:, j : j + 1], None, ALU.mult)
+                for cols in halves if j == 3 else [slice(0, S)]:
+                    nc.vector.tensor_scalar(z_bf[:, cols, j], rows[:, cols], gain[:, j : j + 1], None, ALU.mult)
 
         for t in range(PACK):
-            nc.scalar.activation(ra[t][:], ssum[t][:], ACT.Sqrt)
+            scatter(ub[t], l_n2, rb[t][:])
             if t > 0:
                 finish_z(t - 1)
-            scatter(ub[t], l_n2, rb[t][:])
+            nc.scalar.activation(ra[t][:], ssum[t][:], ACT.Sqrt, bias=quarter[:])
         finish_z(PACK - 1)
 
         z_w = tile("z_w", [P, S], U32)
         z_b = tile("z_b", [P, S], U8)
-        nc.vector.quantize_mx(out=z_w[:].bitcast(FP8X4), scales=z_b[:], in_=z_bf[:].rearrange("p s t -> p (s t)"))
+        for cols in halves:
+            nc.vector.quantize_mx(
+                out=z_w[:, cols].bitcast(FP8X4), scales=z_b[:, cols], in_=z_bf[:, cols, :].rearrange("p s t -> p (s t)")
+            )
 
         far = [tile(f"far_{t}", [P, S], F32) for t in range(PACK)]
         other = [tile(f"other_{t}", [P, S], F32) for t in range(PACK)]
@@ -228,7 +235,11 @@ def tile_picked_atzapolarpagew_none_po_kernel(
         out_rows = out_0.rearrange("(p t) c -> p t c", t=PACK)
 
         def make_h2(t):
-            sixteenth(h2[t][:, :S], product(f"acc2_{t}", second[t], z_w[:], z_b[:]), t == 0)
+            if t == 0:
+                for cols, bank in zip(halves, ("acc1_0", None)):
+                    sixteenth(h2[0][:, cols], product(f"acc2_0_{cols.start}", second[0], z_w[:, cols], z_b[:, cols], bank), True)
+            else:
+                sixteenth(h2[t][:, :S], product(f"acc2_{t}", second[t], z_w[:], z_b[:]), False)
 
         def make_st(t, pieces=1):
             step = S // pieces
@@ -248,7 +259,7 @@ def tile_picked_atzapolarpagew_none_po_kernel(
             for c in range(0, U, step):
                 nc.vector.tensor_copy(out_bf[:, c : c + step, t], page[t][:, c : c + step])
 
-        second.extend(deal(1, 2, 10.5) + deal(2, 4, 12))
+        second.extend(deal(1, 2, 10.5, 10) + deal(2, 4, 11.5, 10.25))
         for t in range(PACK):
             make_h2(t)
         make_st(0)

from contextlib import ExitStack

import concourse.mybir as mybir

F32 = mybir.dt.float32
BF16 = mybir.dt.bfloat16
I32 = mybir.dt.int32
U32 = mybir.dt.uint32
U16 = mybir.dt.uint16
U8 = mybir.dt.uint8
FP8X4 = mybir.dt.float8_e4m3fn_x4
ALU = mybir.AluOpType
ACT = mybir.ActivationFunctionType

P = 128
PACK = 4
K, T, S, G, H, W, U = 512, 1024, 256, 2048, 512, 128, 512
HALF = H // 2
SPARE = 16
KIB = 1024

FLOPS = 4 * 2 * K * H * S


def tile_picked_atzapolarpagew_none_po_kernel(
    tc, x_words, x_scales, d_words, d_scales, gs, offs, ka, kb, n1, n2, kc, kd, n3, n4, n5, n6, out_0, out_1, out_2
):
    nc = tc.nc
    with ExitStack() as ctx:
        keep = ctx.enter_context(tc.tile_pool(name="keep", bufs=1))
        shared = ctx.enter_context(tc.tile_pool(name="shared", bufs=1))
        psum = ctx.enter_context(tc.psum_pool(name="psum", bufs=1))

        def tile(name, shape, dtype, kib=None):
            if kib is None:
                return keep.tile(shape, dtype, name=name, align_bytes=64)
            return shared.tile(shape, dtype, name=name, offset=int(kib * KIB), align_bytes=64)

        def load_list(name, src):
            lst = tile(name, list(src.shape), U16)
            nc.sync.dma_start(lst[:], src)
            return lst

        def load_rows(name, rows):
            dst = tile(name, [P, rows.shape[1]], U8)
            words = rows.bitcast(I32)
            nc.sync.dma_start(dst[:].bitcast(I32), words.unsqueeze(1).broadcast_to([16, 8, words.shape[1]]))
            return dst

        def load_words(name, words):
            dst = tile(name, [P, words.shape[1]], I32)
            nc.sync.dma_start(dst[:], words.rearrange("p n t -> p (n t)").bitcast(I32))
            return dst

        l_ka = load_list("l_ka", ka)
        d_bytes = load_rows("d_bytes", d_scales[0])
        l_kb = load_list("l_kb", kb)
        x_bytes = load_rows("x_bytes", x_scales[0])
        l_offs = load_list("l_offs", offs)
        x_tab = load_words("x_tab", x_words[0])
        d_tab = load_words("d_tab", d_words[0])
        l_n1 = load_list("l_n1", n1)
        l_n2 = load_list("l_n2", n2)
        l_kc = load_list("l_kc", kc)
        l_kd = load_list("l_kd", kd)
        gain = tile("gain", [P, PACK], F32)
        nc.sync.dma_start(gain[:], gs.rearrange("(p t) o -> p (t o)", t=PACK))
        l_n5 = load_list("l_n5", n5)
        l_n6 = load_list("l_n6", n6)
        l_n3 = load_list("l_n3", n3)
        l_n4 = load_list("l_n4", n4)

        warm_in = tile("warm_in", [P, 1], F32)
        warm_out = tile("warm_out", [P, 1], F32)
        nc.vector.memset(warm_in[:], 1.0)
        nc.scalar.activation(warm_out[:], warm_in[:], ACT.Sqrt)

        quarter = tile("quarter", [P, 1], F32)
        nc.vector.memset(quarter[:], 0.25)
        placed1 = tile("placed1", [P, 2 * H + S], U8)
        placed2 = tile("placed2", [P, 2 * H], U8)
        nc.vector.memset(placed1[:].bitcast(I32), 0)
        nc.vector.memset(placed2[:].bitcast(I32), 0)
        h2 = [tile(f"h2_{t}", [P, S + SPARE], F32) for t in range(PACK)]
        st = [tile(f"st_{t}", [P, S + SPARE], F32) for t in range(PACK)]
        for t in range(PACK):
            nc.vector.memset(h2[t][:, S:], 0.0)
            nc.vector.memset(st[t][:, S:], 0.0)

        def pick(out, window, offsets):
            nc.vector.tensor_copy(out, window.indirect(offsets))

        def pick_words(picked, u, lists):
            for l, lst in enumerate(lists):
                pick(picked[:, l * HALF : (l + 1) * HALF], d_tab[:].bitcast(U32), lst[:, 16 * u : 16 * (u + 1)])

        def place(picked, placed, queue):
            for q in range(4):
                queue.dma_start(
                    placed[32 * q : 32 * q + 4, :].bitcast(I32), picked[32 * q : 32 * q + 32 : 8, :].bitcast(I32)
                )

        def deal_low(name, u, picked, placed):
            w = tile(f"{name}_w{u}", [P, 2, P], U32)
            b = tile(f"{name}_b{u}", [P, 2, P], U8)
            words = picked[:].rearrange("p (l m t) -> p l m t", l=2, t=PACK)
            scales = placed[:, : 2 * H].rearrange("p (l u m t) -> p u l m t", l=2, u=2, t=PACK)[:, u]
            for dst, src in ((w, words), (b, scales)):
                nc.vector.tensor_copy(dst[:].rearrange("p l (t m) -> p l m t", t=2), src[:, :, :, 0:2])
            return w[:], b[:]

        def deal_high(name, picked, placed, kib=None):
            w = tile(f"{name}_w23", [P, 2, 2, P], U32, kib)
            b = tile(f"{name}_b23", [P, 2, 2, P], U8, kib and kib - 0.5)
            for u in range(2):
                words = picked[u][:].rearrange("p (l m t) -> p l m t", l=2, t=PACK)
                nc.vector.tensor_copy(w[:, :, :, 64 * u : 64 * (u + 1)].rearrange("p t l m -> p l m t"), words[:, :, :, 2:4])
            scales = placed[:, : 2 * H].rearrange("p (m t) -> p m t", t=PACK)
            nc.vector.tensor_copy(b[:].rearrange("p t l m -> p (l m) t"), scales[:, :, 2:4])
            return [(w[:, t], b[:, t]) for t in range(2)]

        def product(name, stationary, rhs_w, rhs_b, bank=None):
            w, b = stationary
            acc = psum.tile([P, rhs_w.shape[1]], F32, name=name, tag=bank or name)
            for l in range(2):
                nc.tensor.matmul_mx(
                    out=acc[:], lhsT=w[:, l, :].bitcast(FP8X4), lhsT_scale=b[:, l, :],
                    rhs=rhs_w.bitcast(FP8X4), rhs_scale=rhs_b, start=(l == 0), stop=(l == 1),
                )
            return acc

        def sixteenth(dst, acc, on_scalar):
            if on_scalar:
                nc.scalar.activation(dst, acc[:], ACT.Copy, scale=0.0625)
            else:
                nc.vector.tensor_scalar(dst, acc[:], 0.0625, None, ALU.mult)

        def fetch(out, window, offsets):
            nc.scalar.activation(out, window[:].indirect(offsets), ACT.Copy)

        def scatter(window, lst, values):
            nc.scalar.activation(window[:].indirect(lst[:]), values, ACT.Copy)

        def swap_halves(u, src, planes):
            for j in range(2):
                nc.sync.dma_start(planes[64 * u : 64 * (u + 1), j, :], src[64 * j : 64 * (j + 1), :])

        picked_b1 = tile("picked_b1", [P, 2 * H + S], U8, 0)
        pick(picked_b1[:, 0:H], d_bytes[:], l_ka[:])
        pick(picked_b1[:, H : 2 * H], d_bytes[:], l_kb[:])
        pick(picked_b1[:, 2 * H :], x_bytes[:], l_offs[:])
        place(picked_b1, placed1, nc.scalar)
        x_picked = tile("x_picked", [P, S], U32)
        pick(x_picked[:], x_tab[:].bitcast(U32), l_offs[:])
        picked_w1 = [tile("picked_w1_0", [P, H], U32), tile("picked_w1_1", [P, H], U32, 0)]
        acc1 = []
        for u in range(2):
            pick_words(picked_w1[u], u, (l_ka, l_kb))
            acc1.append(product(f"acc1_{u}", deal_low("first", u, picked_w1[u], placed1), x_picked[:], placed1[:, 2 * H :]))
        for t, stationary in enumerate(deal_high("first", picked_w1, placed1), 2):
            acc1.append(product(f"acc1_{t}", stationary, x_picked[:], placed1[:, 2 * H :]))

        h = [tile(f"h_{t}", [P, S], F32) for t in range(PACK)]
        pab = [tile(f"pab_{t}", [P, 2 * W], F32, (2, 4, 6, 34)[t]) for t in range(PACK)]
        rb = [tile(f"rb_{t}", [P, W], F32) for t in range(PACK)]
        ra = [tile(f"ra_{t}", [P, W], F32) for t in range(PACK)]
        ssum = [tile(f"ssum_{t}", [P, W], F32) for t in range(PACK)]
        sq = [tile(f"sq_{t}", [P, 2 * W], F32) for t in range(PACK)]
        ub = [tile(f"ub_{t}", [P, S], F32, (10, 11, 15, 16)[t]) for t in range(PACK)]
        for t in range(PACK):
            sixteenth(h[t][:], acc1[t], t < 2)
            fetch(pab[t][:, :W], h[t], l_n1[:])
            fetch(pab[t][:, W:], h[t], l_n2[:])

        def polar(t):
            nc.vector.scalar_tensor_tensor(rb[t][:], pab[t][:, :W], -0.5, pab[t][:, W:], ALU.mult, ALU.add)
            nc.gpsimd.tensor_tensor(sq[t][:], pab[t][:], pab[t][:], ALU.mult)
            nc.gpsimd.tensor_tensor(ssum[t][:], sq[t][:, :W], sq[t][:, W:], ALU.add)

        polar(0)
        polar(1)
        picked_b2 = tile("picked_b2", [P, 2 * H], U8, 4)
        pick(picked_b2[:, 0:H], d_bytes[:], l_kc[:])
        pick(picked_b2[:, H:], d_bytes[:], l_kd[:])
        place(picked_b2, placed2, nc.sync)
        polar(2)
        polar(3)
        picked_w2 = tile("picked_w2", [P, 2 * H], U32, 34)
        pick(picked_w2[:, 0:H], d_tab[:].bitcast(U32), l_kc[:])
        pick(picked_w2[:, H:], d_tab[:].bitcast(U32), l_kd[:])

        def deal(t0, t1, kib=None, kib_b=None):
            w = tile(f"second_w{t0}", [P, t1 - t0, 2, P], U32, kib and kib + 0.25)
            b = tile(f"second_b{t0}", [P, t1 - t0, 2, P], U8, kib_b)
            for dst, src in ((w, picked_w2), (b, placed2)):
                nc.vector.tensor_copy(
                    dst[:].rearrange("p t l m -> p (l m) t"), src[:].rearrange("p (m t) -> p m t", t=PACK)[:, :, t0:t1]
                )
            return [(w[:, t], b[:, t]) for t in range(t1 - t0)]

        second = deal(0, 1)

        halves = [slice(0, S // 2), slice(S // 2, S)]
        ub_low = tile("ub_low", [P, 2, S], F32)
        z_bf = tile("z_bf", [P, S, PACK], BF16, 10)

        def finish_z(t):
            scatter(ub[t], l_n1, ra[t][:])
            if t < 2:
                swap_halves(t, ub[t], ub_low)
            for j in ((), (0, 1), (2,), (3,))[t]:
                rows = ub_low[:, j, :] if j < 2 else ub[j][:]
                for cols in halves if j == 3 else [slice(0, S)]:
                    nc.vector.tensor_scalar(z_bf[:, cols, j], rows[:, cols], gain[:, j : j + 1], None, ALU.mult)

        for t in range(PACK):
            scatter(ub[t], l_n2, rb[t][:])
            if t > 0:
                finish_z(t - 1)
            nc.scalar.activation(ra[t][:], ssum[t][:], ACT.Sqrt, bias=quarter[:])
        finish_z(PACK - 1)

        z_w = tile("z_w", [P, S], U32)
        z_b = tile("z_b", [P, S], U8)
        for cols in halves:
            nc.vector.quantize_mx(
                out=z_w[:, cols].bitcast(FP8X4), scales=z_b[:, cols], in_=z_bf[:, cols, :].rearrange("p s t -> p (s t)")
            )

        far = [tile(f"far_{t}", [P, S], F32) for t in range(PACK)]
        other = [tile(f"other_{t}", [P, S], F32) for t in range(PACK)]
        up = [tile(f"up_{t}", [P, S], F32) for t in range(PACK)]
        page = [tile(f"page_{t}", [P, U], F32) for t in range(PACK)]
        out_bf = tile("out_bf", [P, U, PACK], BF16)
        out_rows = out_0.rearrange("(p t) c -> p t c", t=PACK)

        def make_h2(t):
            if t == 0:
                for cols, bank in zip(halves, ("acc1_0", None)):
                    sixteenth(h2[0][:, cols], product(f"acc2_0_{cols.start}", second[0], z_w[:, cols], z_b[:, cols], bank), True)
            else:
                sixteenth(h2[t][:, :S], product(f"acc2_{t}", second[t], z_w[:], z_b[:]), False)

        def make_st(t, pieces=1):
            step = S // pieces
            for c in range(0, S, step):
                fetch(far[t][:, c : c + step], h2[t], l_n5[:, c // 16 : (c + step) // 16])
                nc.vector.tensor_tensor(st[t][:, c : c + step], h2[t][:, c : c + step], far[t][:, c : c + step], ALU.subtract)

        def make_up(t):
            fetch(other[t][:], st[t], l_n6[:])
            nc.vector.tensor_tensor(up[t][:], st[t][:, :S], other[t][:], ALU.max)
            scatter(page[t], l_n3, st[t][:, :S])

        def finish_page(t, pieces=1):
            scatter(page[t], l_n4, up[t][:])
            nc.sync.dma_start(out_rows[:, t, :], page[t][:])
            step = U // pieces
            for c in range(0, U, step):
                nc.vector.tensor_copy(out_bf[:, c : c + step, t], page[t][:, c : c + step])

        second.extend(deal(1, 2, 10.5, 10) + deal(2, 4, 11.5, 10.25))
        for t in range(PACK):
            make_h2(t)
        make_st(0)
        make_st(1)
        make_up(0)
        make_st(2)
        finish_page(0)
        make_up(1)
        make_st(3)
        finish_page(1)
        make_up(2)
        make_up(3)
        finish_page(2)
        finish_page(3, 2)

        out_w = tile("out_w", [P, U], U32)
        out_b = tile("out_b", [P, U], U8)
        words_dram = out_1[0].rearrange("p n t -> p (n t)").bitcast(I32)
        half = U // 2
        for c in range(0, U, half):
            nc.vector.quantize_mx(
                out=out_w[:, c : c + half].bitcast(FP8X4), scales=out_b[:, c : c + half],
                in_=out_bf[:, c : c + half, :].rearrange("p s t -> p (s t)"),
            )
            nc.sync.dma_start(words_dram[:, c : c + half], out_w[:, c : c + half].bitcast(I32))
        for q in range(4):
            (nc.scalar, nc.sync)[q // 3].dma_start(out_2[0, 4 * q : 4 * q + 4, :].bitcast(I32), out_b[32 * q : 32 * q + 4, :].bitcast(I32))
